import numpy as np
import ml_dtypes


def mxq(x, axis, fmt="e4m3"):
    dtype, down = {"e4m3": (ml_dtypes.float8_e4m3fn, 7), "e5m2": (ml_dtypes.float8_e5m2, 14)}[fmt]
    v = np.moveaxis(np.asarray(x, np.float32).astype(ml_dtypes.bfloat16).astype(np.float64), axis, -1)
    blocks = v.reshape(v.shape[:-1] + (-1, 32))
    amax = np.abs(blocks).max(-1, keepdims=True)
    byte = np.maximum(np.where(amax > 0, np.frexp(amax)[1] - 1 + 127, 0) - down, 1)
    scale = np.exp2(byte - 127.0)
    codes = (blocks / scale).astype(np.float32).astype(dtype).astype(np.float64)
    return np.moveaxis((codes * scale).reshape(v.shape), -1, axis)


WIDE = False


def mx_kscale(k):
    if not WIDE:
        return np.ones(k)
    levels = np.array([10, -10, 5, -5, 0])
    if k % 512:
        return np.exp2(np.random.permutation(np.resize(levels, k // 32))).repeat(32)
    a = np.empty((k // 512, 16))
    for p in range(k // 512):
        a[p, :8] = np.random.permutation(np.resize(levels, 8))
        for g in range(8):
            far = levels[np.abs(levels - a[p, g]) >= 10]
            a[p, g + 8] = far[np.random.randint(len(far))]
    return np.exp2(a.ravel()).repeat(32)


def f64(x):
    return np.asarray(x).astype(np.float64)


def striped(idx):
    return np.tile(np.asarray(idx).reshape(-1, 16).T, (8, 1)).astype(np.uint16)


def unstriped(offs):
    return offs[:16].T.reshape(-1).astype(np.int64)


E2M1 = np.array([0.0, 0.5, 1.0, 1.5, 2.0, 3.0, 4.0, 6.0, -0.0, -0.5, -1.0, -1.5, -2.0, -3.0, -4.0, -6.0])


def pack_weight(w, fmt):
    k, n = w.shape
    w = f64(np.asarray(w, np.float32).astype(ml_dtypes.bfloat16)).reshape(k // 32, 32, n)
    amax = np.abs(w).max(1)
    if fmt == "e4m3":
        byte = np.frexp(amax)[1] - 1 + 127 - 7
    else:
        mant, ex = np.frexp(amax / 6.0)
        byte = np.where(mant > 0.5, ex, ex - 1) + 127
    byte = np.clip(np.where(amax > 0, byte, 1), 1, 254)
    scaled = (w * np.exp2(127.0 - byte)[:, None, :]).reshape(k, n).astype(np.float32)
    by_word = np.ascontiguousarray(scaled.reshape(k // 512, 128, 4, n).transpose(0, 1, 3, 2))
    if fmt == "e4m3":
        words = by_word.astype(ml_dtypes.float8_e4m3fn).view(np.uint8)
    else:
        c = by_word.astype(ml_dtypes.float4_e2m1fn).view(np.uint8) & 0xF
        words = (c[..., 0::2] | (c[..., 1::2] << 4)).reshape(k // 512, 128, 2 * n)
    return np.ascontiguousarray(words), np.ascontiguousarray(byte.astype(np.uint8).reshape(k // 512, 16, n))


def unpack_weight(words, scales, fmt):
    g, _, n = scales.shape
    words = np.ascontiguousarray(words).reshape(g, 128, n, -1)
    if fmt == "e4m3":
        vals = words.view(ml_dtypes.float8_e4m3fn).astype(np.float64)
    else:
        nib = np.empty((g, 128, n, 4), np.uint8)
        nib[..., 0::2] = words & 0xF
        nib[..., 1::2] = words >> 4
        vals = E2M1[nib]
    vals = vals * np.repeat(np.exp2(scales.astype(np.float64) - 127.0), 8, axis=1)[..., None]
    return vals.transpose(0, 1, 3, 2).reshape(g * 512, n)


B, N, T, D, NQ = 1, 512, 2048, 512, 256


def setup_inputs():
    n = np.random.standard_normal
    idx = np.sort(np.random.permutation(T)[:B * N].reshape(B, N), axis=1).reshape(-1)
    s = mx_kscale(D)[:, None]
    kp = pack_weight(n((D, T)) / s, "e4m3")
    return {
        "qT": (n((B, D, NQ)) * s * (1.00 / np.sqrt(D))).astype(np.float32),
        "k_words": kp[0],
        "k_scales": kp[1],
        "dm": (np.where(np.random.uniform(size=(B, NQ, N)) < 0.9, 1.0 / 0.9, 0.0)).astype(np.float32),
        "offs": striped(idx),
    }


def reference(qT, k_words, k_scales, dm, offs):
    idx = unstriped(offs)
    pick = lambda x, which: x[:, which].reshape(x.shape[0], B, -1).transpose(1, 0, 2)
    k = unpack_weight(k_words, k_scales, "e4m3")
    kg = pick(k, idx)
    qq = mxq(f64(qT), 1, "e4m3")
    a = qq.transpose(0, 2, 1) @ kg
    m = np.max(a, axis=-1, keepdims=True)
    e = np.exp(a - m)
    l = np.sum(e, axis=-1, keepdims=True)
    y = e / l * f64(dm)
    return y

@@ -1,0 +1,118 @@
+from contextlib import ExitStack
+
+import concourse.mybir as mybir
+
+F32 = mybir.dt.float32
+BF16 = mybir.dt.bfloat16
+I32 = mybir.dt.int32
+U32 = mybir.dt.uint32
+U16 = mybir.dt.uint16
+U8 = mybir.dt.uint8
+FP8X4 = mybir.dt.float8_e4m3fn_x4
+ALU = mybir.AluOpType
+ACT = mybir.ActivationFunctionType
+
+P = 128
+PACK = 4
+T = 2048
+D = 512
+NQ = 256
+N = 512
+HALF = N // 2
+PREFIX = T - HALF
+Q_TILES = NQ // P
+
+FLOPS = 2 * NQ * N * D
+
+
+def tile_attend_wtdrop_srt_kernel(tc, qT, k_words, k_scales, dm, offs, out):
+    nc = tc.nc
+    with ExitStack() as ctx:
+        sb = ctx.enter_context(tc.tile_pool(name="sb", bufs=1))
+        psum = ctx.enter_context(tc.psum_pool(name="psum", bufs=1))
+
+        pool_scales = sb.tile([P, T], U8, name="pool_scales", align_bytes=64)
+        nc.vector.memset(pool_scales[:].bitcast(I32), 0)
+        warm = sb.tile([P, 8], F32, name="warm")
+        nc.vector.memset(warm[:], 0.0)
+
+        scale_rows = k_scales[0].bitcast(I32)
+        for r in range(4):
+            nc.scalar.dma_start(out=pool_scales[r:P:32, :].bitcast(I32), in_=scale_rows[r:16:4, :])
+
+        q_raw = sb.tile([P, PACK, NQ], F32, name="q_raw")
+        nc.sync.dma_start(out=q_raw[:], in_=qT[0].rearrange("(p j) w -> p j w", j=PACK))
+        offsets = sb.tile([P, N // 16], U16, name="offsets")
+        nc.sync.dma_start(offsets[:], offs)
+        pool_words = sb.tile([P, T], I32, name="pool_words", align_bytes=64)
+        word_rows = k_words[0].rearrange("p n t -> p (n t)").bitcast(I32)
+        nc.sync.dma_start(out=pool_words[:, :PREFIX], in_=word_rows[:, :PREFIX])
+        nc.sync.dma_start(out=pool_words[:, PREFIX:], in_=word_rows[:, PREFIX:])
+        drop = sb.tile([P, Q_TILES, N], F32, name="drop")
+        nc.sync.dma_start(out=drop[:], in_=dm[0].rearrange("(t p) n -> p t n", p=P))
+
+        warm_out = sb.tile([P, 8], F32, name="warm_out")
+        nc.scalar.activation(warm_out[:], warm[:], ACT.Exp)
+
+        q_bf = sb.tile([P, NQ, PACK], BF16, name="q_bf", align_bytes=64)
+        nc.vector.tensor_copy(
+            out=q_bf[:].rearrange("p (c i) j -> p c j i", i=4),
+            in_=q_raw[:].rearrange("p j (c i) -> p c j i", i=4),
+        )
+        q_codes = sb.tile([P, NQ], U32, name="q_codes", align_bytes=64)
+        q_scales = sb.tile([P, NQ], U8, name="q_scales", align_bytes=64)
+        nc.vector.quantize_mx(
+            out=q_codes[:].bitcast(FP8X4), scales=q_scales[:], in_=q_bf[:].rearrange("p w j -> p (w j)")
+        )
+
+        key_scales = sb.tile([P, N], U8, name="key_scales", align_bytes=64)
+        nc.vector.tensor_copy(key_scales[:], pool_scales[:].indirect(offsets[:]))
+
+        key_words = []
+        for h, width in enumerate((PREFIX, T)):
+            kw = sb.tile([P, HALF], U32, name=f"key_words{h}", align_bytes=64)
+            cols = slice(h * HALF // 16, (h + 1) * HALF // 16)
+            nc.vector.tensor_copy(kw[:], pool_words[:, :width].bitcast(U32).indirect(offsets[:, cols]))
+            key_words.append(kw)
+
+        neg = [sb.tile([P, N], F32, name=f"neg{t}") for t in range(Q_TILES)]
+        neg_max = [[sb.tile([P, 1], F32, name=f"neg_max{t}_{h}") for h in range(2)] for t in range(Q_TILES)]
+        for h in range(2):
+            slots = slice(h * HALF, (h + 1) * HALF)
+            for t in range(Q_TILES):
+                rows = slice(t * P, (t + 1) * P)
+                bank = psum.tile([P, N], F32, name=f"bank{t}_{h}")
+                nc.tensor.matmul_mx(
+                    out=bank[:, :HALF],
+                    lhsT=q_codes[:, rows].bitcast(FP8X4),
+                    lhsT_scale=q_scales[:, rows],
+                    rhs=key_words[h][:].bitcast(FP8X4),
+                    rhs_scale=key_scales[:, slots],
+                    start=True,
+                    stop=True,
+                )
+                nc.vector.tensor_scalar(
+                    out=neg[t][:, slots],
+                    in0=bank[:, :HALF],
+                    scalar1=-1.0,
+                    scalar2=neg_max[t][0][:] if h else None,
+                    op0=ALU.mult,
+                    op1=ALU.min,
+                    accum_out=neg_max[t][h][:],
+                )
+
+        for t in range(Q_TILES):
+            rows = slice(t * P, (t + 1) * P)
+            e = sb.tile([P, N], F32, name=f"e{t}")
+            row_sum = sb.tile([P, 1], F32, name=f"row_sum{t}")
+            nc.scalar.activation(e[:], neg[t][:], ACT.Exp, bias=neg_max[t][1][:], scale=-1.0, accum_out=row_sum[:])
+            inv = sb.tile([P, 1], F32, name=f"inv{t}")
+            nc.vector.reciprocal(inv[:], row_sum[:])
+            for h in range(2):
+                slots = slice(h * HALF, (h + 1) * HALF)
+                y = sb.tile([P, HALF], F32, name=f"y{t}_{h}")
+                nc.vector.scalar_tensor_tensor(
+                    out=y[:], in0=e[:, slots], scalar=inv[:], in1=drop[:, t, slots], op0=ALU.mult, op1=ALU.mult
+                )
+                queue = nc.scalar if h else nc.sync
+                queue.dma_start(out=out[0, rows, slots], in_=y[:])

@@ -31,34 +31,30 @@ def tile_attend_wtdrop_srt_kernel(tc, qT, k_words, k_scales, dm, offs, out):
         sb = ctx.enter_context(tc.tile_pool(name="sb", bufs=1))
         psum = ctx.enter_context(tc.psum_pool(name="psum", bufs=1))
 
-        pool_scales = sb.tile([P, T], U8, name="pool_scales", align_bytes=64)
+        pool_scales = sb.tile([P, T], U8, name="pool_scales", tag="key_words0", align_bytes=64)
         nc.vector.memset(pool_scales[:].bitcast(I32), 0)
-        warm = sb.tile([P, 8], F32, name="warm")
-        nc.vector.memset(warm[:], 0.0)
 
-        scale_rows = k_scales[0].bitcast(I32)
-        for r in range(4):
-            nc.scalar.dma_start(out=pool_scales[r:P:32, :].bitcast(I32), in_=scale_rows[r:16:4, :])
-
-        q_raw = sb.tile([P, PACK, NQ], F32, name="q_raw")
+        q_raw = sb.tile([P, PACK, NQ], F32, name="q_raw", tag="staged")
         nc.sync.dma_start(out=q_raw[:], in_=qT[0].rearrange("(p j) w -> p j w", j=PACK))
         offsets = sb.tile([P, N // 16], U16, name="offsets")
         nc.sync.dma_start(offsets[:], offs)
+        scale_rows = k_scales[0].bitcast(I32)
+        for r in range(4):
+            nc.sync.dma_start(out=pool_scales[r:P:32, :].bitcast(I32), in_=scale_rows[r:16:4, :])
+
         pool_words = sb.tile([P, T], I32, name="pool_words", align_bytes=64)
         word_rows = k_words[0].rearrange("p n t -> p (n t)").bitcast(I32)
         nc.sync.dma_start(out=pool_words[:, :PREFIX], in_=word_rows[:, :PREFIX])
         nc.sync.dma_start(out=pool_words[:, PREFIX:], in_=word_rows[:, PREFIX:])
-        drop = sb.tile([P, Q_TILES, N], F32, name="drop")
-        nc.sync.dma_start(out=drop[:], in_=dm[0].rearrange("(t p) n -> p t n", p=P))
-
-        warm_out = sb.tile([P, 8], F32, name="warm_out")
-        nc.scalar.activation(warm_out[:], warm[:], ACT.Exp)
 
         q_bf = sb.tile([P, NQ, PACK], BF16, name="q_bf", align_bytes=64)
-        nc.vector.tensor_copy(
-            out=q_bf[:].rearrange("p (c i) j -> p c j i", i=4),
-            in_=q_raw[:].rearrange("p j (c i) -> p c j i", i=4),
-        )
+        for copy, cols in ((nc.vector.tensor_copy, slice(0, P)), (nc.scalar.copy, slice(P, NQ))):
+            copy(
+                out=q_bf[:, cols, :].rearrange("p (c i) j -> p c j i", i=4),
+                in_=q_raw[:, :, cols].rearrange("p j (c i) -> p c j i", i=4),
+            )
+        drop = sb.tile([P, Q_TILES, N], F32, name="drop", tag="staged")
+        nc.sync.dma_start(out=drop[:], in_=dm[0].rearrange("(t p) n -> p t n", p=P))
         q_codes = sb.tile([P, NQ], U32, name="q_codes", align_bytes=64)
         q_scales = sb.tile([P, NQ], U8, name="q_scales", align_bytes=64)
         nc.vector.quantize_mx(
@@ -70,17 +66,17 @@ def tile_attend_wtdrop_srt_kernel(tc, qT, k_words, k_scales, dm, offs, out):
 
         key_words = []
         for h, width in enumerate((PREFIX, T)):
-            kw = sb.tile([P, HALF], U32, name=f"key_words{h}", align_bytes=64)
+            kw = sb.tile([P, HALF], U32, name=f"key_words{h}", tag=f"key_words{h}", align_bytes=64)
             cols = slice(h * HALF // 16, (h + 1) * HALF // 16)
             nc.vector.tensor_copy(kw[:], pool_words[:, :width].bitcast(U32).indirect(offsets[:, cols]))
             key_words.append(kw)
 
         neg = [sb.tile([P, N], F32, name=f"neg{t}") for t in range(Q_TILES)]
         neg_max = [[sb.tile([P, 1], F32, name=f"neg_max{t}_{h}") for h in range(2)] for t in range(Q_TILES)]
-        for h in range(2):
-            slots = slice(h * HALF, (h + 1) * HALF)
-            for t in range(Q_TILES):
-                rows = slice(t * P, (t + 1) * P)
+        for t in range(Q_TILES):
+            rows = slice(t * P, (t + 1) * P)
+            for h in range(2):
+                slots = slice(h * HALF, (h + 1) * HALF)
                 bank = psum.tile([P, N], F32, name=f"bank{t}_{h}")
                 nc.tensor.matmul_mx(
                     out=bank[:, :HALF],
@@ -111,8 +107,13 @@ def tile_attend_wtdrop_srt_kernel(tc, qT, k_words, k_scales, dm, offs, out):
             for h in range(2):
                 slots = slice(h * HALF, (h + 1) * HALF)
                 y = sb.tile([P, HALF], F32, name=f"y{t}_{h}")
-                nc.vector.scalar_tensor_tensor(
-                    out=y[:], in0=e[:, slots], scalar=inv[:], in1=drop[:, t, slots], op0=ALU.mult, op1=ALU.mult
-                )
-                queue = nc.scalar if h else nc.sync
+                if (t, h) == (0, 0):
+                    kept = sb.tile([P, HALF], F32, name="kept")
+                    nc.vector.tensor_tensor(kept[:], e[:, slots], drop[:, t, slots], ALU.mult)
+                    nc.scalar.activation(y[:], kept[:], ACT.Copy, scale=inv[:])
+                else:
+                    nc.vector.scalar_tensor_tensor(
+                        out=y[:], in0=e[:, slots], scalar=inv[:], in1=drop[:, t, slots], op0=ALU.mult, op1=ALU.mult
+                    )
+                queue = nc.scalar if t == h else nc.sync
                 queue.dma_start(out=out[0, rows, slots], in_=y[:])

@@ -40,26 +40,30 @@ def tile_attend_wtdrop_srt_kernel(tc, qT, k_words, k_scales, dm, offs, out):
         nc.sync.dma_start(offsets[:], offs)
         scale_rows = k_scales[0].bitcast(I32)
         for r in range(4):
-            nc.sync.dma_start(out=pool_scales[r:P:32, :].bitcast(I32), in_=scale_rows[r:16:4, :])
+            queue = nc.scalar if r % 2 else nc.sync
+            queue.dma_start(out=pool_scales[r:P:32, :].bitcast(I32), in_=scale_rows[r:16:4, :])
 
         pool_words = sb.tile([P, T], I32, name="pool_words", align_bytes=64)
         word_rows = k_words[0].rearrange("p n t -> p (n t)").bitcast(I32)
         nc.sync.dma_start(out=pool_words[:, :PREFIX], in_=word_rows[:, :PREFIX])
         nc.sync.dma_start(out=pool_words[:, PREFIX:], in_=word_rows[:, PREFIX:])
 
-        q_bf = sb.tile([P, NQ, PACK], BF16, name="q_bf", align_bytes=64)
-        for copy, cols in ((nc.vector.tensor_copy, slice(0, P)), (nc.scalar.copy, slice(P, NQ))):
-            copy(
-                out=q_bf[:, cols, :].rearrange("p (c i) j -> p c j i", i=4),
-                in_=q_raw[:, :, cols].rearrange("p j (c i) -> p c j i", i=4),
+        q_codes, q_scales = [], []
+        for t, cast in enumerate((nc.vector.tensor_copy, nc.scalar.copy)):
+            q_bf = sb.tile([P, P, PACK], BF16, name=f"q_bf{t}", align_bytes=64)
+            cast(
+                out=q_bf[:].rearrange("p (c i) j -> p c j i", i=4),
+                in_=q_raw[:, :, t * P : (t + 1) * P].rearrange("p j (c i) -> p c j i", i=4),
             )
+            codes = sb.tile([P, P], U32, name=f"q_codes{t}", align_bytes=64)
+            scales = sb.tile([P, P], U8, name=f"q_scales{t}", align_bytes=64)
+            nc.vector.quantize_mx(
+                out=codes[:].bitcast(FP8X4), scales=scales[:], in_=q_bf[:].rearrange("p w j -> p (w j)")
+            )
+            q_codes.append(codes)
+            q_scales.append(scales)
         drop = sb.tile([P, Q_TILES, N], F32, name="drop", tag="staged")
         nc.sync.dma_start(out=drop[:], in_=dm[0].rearrange("(t p) n -> p t n", p=P))
-        q_codes = sb.tile([P, NQ], U32, name="q_codes", align_bytes=64)
-        q_scales = sb.tile([P, NQ], U8, name="q_scales", align_bytes=64)
-        nc.vector.quantize_mx(
-            out=q_codes[:].bitcast(FP8X4), scales=q_scales[:], in_=q_bf[:].rearrange("p w j -> p (w j)")
-        )
 
         key_scales = sb.tile([P, N], U8, name="key_scales", align_bytes=64)
         nc.vector.tensor_copy(key_scales[:], pool_scales[:].indirect(offsets[:]))
@@ -80,8 +84,8 @@ def tile_attend_wtdrop_srt_kernel(tc, qT, k_words, k_scales, dm, offs, out):
                 bank = psum.tile([P, N], F32, name=f"bank{t}_{h}")
                 nc.tensor.matmul_mx(
                     out=bank[:, :HALF],
-                    lhsT=q_codes[:, rows].bitcast(FP8X4),
-                    lhsT_scale=q_scales[:, rows],
+                    lhsT=q_codes[t][:].bitcast(FP8X4),
+                    lhsT_scale=q_scales[t][:],
                     rhs=key_words[h][:].bitcast(FP8X4),
                     rhs_scale=key_scales[:, slots],
                     start=True,

@@ -108,16 +108,17 @@ def tile_attend_wtdrop_srt_kernel(tc, qT, k_words, k_scales, dm, offs, out):
             nc.scalar.activation(e[:], neg[t][:], ACT.Exp, bias=neg_max[t][1][:], scale=-1.0, accum_out=row_sum[:])
             inv = sb.tile([P, 1], F32, name=f"inv{t}")
             nc.vector.reciprocal(inv[:], row_sum[:])
-            for h in range(2):
-                slots = slice(h * HALF, (h + 1) * HALF)
-                y = sb.tile([P, HALF], F32, name=f"y{t}_{h}")
-                if (t, h) == (0, 0):
-                    kept = sb.tile([P, HALF], F32, name="kept")
+            cuts = ((0, 192, 320, 512), (0, 128, 320, 512))[t]
+            for lo, hi in zip(cuts, cuts[1:]):
+                slots = slice(lo, hi)
+                y = sb.tile([P, hi - lo], F32, name=f"y{t}_{lo}")
+                if lo == 0:
+                    kept = sb.tile([P, hi], F32, name=f"kept{t}")
                     nc.vector.tensor_tensor(kept[:], e[:, slots], drop[:, t, slots], ALU.mult)
                     nc.scalar.activation(y[:], kept[:], ACT.Copy, scale=inv[:])
+                    nc.scalar.dma_start(out=out[0, rows, slots], in_=y[:])
                 else:
                     nc.vector.scalar_tensor_tensor(
                         out=y[:], in0=e[:, slots], scalar=inv[:], in1=drop[:, t, slots], op0=ALU.mult, op1=ALU.mult
                     )
-                queue = nc.scalar if t == h else nc.sync
-                queue.dma_start(out=out[0, rows, slots], in_=y[:])
+                    nc.sync.dma_start(out=out[0, rows, slots], in_=y[:])

@@ -31,25 +31,30 @@ def tile_attend_wtdrop_srt_kernel(tc, qT, k_words, k_scales, dm, offs, out):
         sb = ctx.enter_context(tc.tile_pool(name="sb", bufs=1))
         psum = ctx.enter_context(tc.psum_pool(name="psum", bufs=1))
 
-        pool_scales = sb.tile([P, T], U8, name="pool_scales", tag="key_words0", align_bytes=64)
-        nc.vector.memset(pool_scales[:].bitcast(I32), 0)
-
-        q_raw = sb.tile([P, PACK, NQ], F32, name="q_raw", tag="staged")
-        nc.sync.dma_start(out=q_raw[:], in_=qT[0].rearrange("(p j) w -> p j w", j=PACK))
+        pool_scales = sb.tile([P, T], U8, name="pool_scales", align_bytes=64)
+        nc.scalar.dma_start(out=pool_scales[16:32, :].bitcast(I32), in_=k_scales[0].bitcast(I32))
+        for lo, hi in ((0, 16), (32, 64), (64, P)):
+            nc.vector.memset(pool_scales[lo:hi, :].bitcast(I32), 0)
         offsets = sb.tile([P, N // 16], U16, name="offsets")
         nc.sync.dma_start(offsets[:], offs)
-        scale_rows = k_scales[0].bitcast(I32)
-        for r in range(4):
-            queue = nc.scalar if r % 2 else nc.sync
-            queue.dma_start(out=pool_scales[r:P:32, :].bitcast(I32), in_=scale_rows[r:16:4, :])
+        q_raw = sb.tile([P, PACK, NQ], F32, name="q_raw", tag="staged")
+        nc.sync.dma_start(out=q_raw[:], in_=qT[0].rearrange("(p j) w -> p j w", j=PACK))
 
         pool_words = sb.tile([P, T], I32, name="pool_words", align_bytes=64)
         word_rows = k_words[0].rearrange("p n t -> p (n t)").bitcast(I32)
         nc.sync.dma_start(out=pool_words[:, :PREFIX], in_=word_rows[:, :PREFIX])
         nc.sync.dma_start(out=pool_words[:, PREFIX:], in_=word_rows[:, PREFIX:])
 
+        spread_scales = sb.tile([P, N], U8, name="spread_scales", align_bytes=64)
+        nc.vector.tensor_copy(spread_scales[:], pool_scales[:].indirect(offsets[:]))
+        key_scales = sb.tile([P, N], U8, name="key_scales", align_bytes=64)
+        nc.vector.memset(key_scales[:].bitcast(I32), 0)
+        for r in range(4):
+            queue = nc.scalar if r % 2 else nc.sync
+            queue.dma_start(out=key_scales[r:P:32, :].bitcast(I32), in_=spread_scales[16 + r : 32 : 4, :].bitcast(I32))
+
         q_codes, q_scales = [], []
-        for t, cast in enumerate((nc.vector.tensor_copy, nc.scalar.copy)):
+        for t, cast in enumerate((nc.vector.tensor_copy, nc.vector.tensor_copy)):
             q_bf = sb.tile([P, P, PACK], BF16, name=f"q_bf{t}", align_bytes=64)
             cast(
                 out=q_bf[:].rearrange("p (c i) j -> p c j i", i=4),
@@ -65,8 +70,6 @@ def tile_attend_wtdrop_srt_kernel(tc, qT, k_words, k_scales, dm, offs, out):
         drop = sb.tile([P, Q_TILES, N], F32, name="drop", tag="staged")
         nc.sync.dma_start(out=drop[:], in_=dm[0].rearrange("(t p) n -> p t n", p=P))
 
-        key_scales = sb.tile([P, N], U8, name="key_scales", align_bytes=64)
-        nc.vector.tensor_copy(key_scales[:], pool_scales[:].indirect(offsets[:]))
 
         key_words = []
         for h, width in enumerate((PREFIX, T)):
@@ -77,11 +80,12 @@ def tile_attend_wtdrop_srt_kernel(tc, qT, k_words, k_scales, dm, offs, out):
 
         neg = [sb.tile([P, N], F32, name=f"neg{t}") for t in range(Q_TILES)]
         neg_max = [[sb.tile([P, 1], F32, name=f"neg_max{t}_{h}") for h in range(2)] for t in range(Q_TILES)]
-        for t in range(Q_TILES):
-            rows = slice(t * P, (t + 1) * P)
-            for h in range(2):
-                slots = slice(h * HALF, (h + 1) * HALF)
+        banks = {}
+        for h in range(2):
+            slots = slice(h * HALF, (h + 1) * HALF)
+            for t in range(Q_TILES):
                 bank = psum.tile([P, N], F32, name=f"bank{t}_{h}")
+                banks[t, h] = bank
                 nc.tensor.matmul_mx(
                     out=bank[:, :HALF],
                     lhsT=q_codes[t][:].bitcast(FP8X4),
@@ -91,9 +95,12 @@ def tile_attend_wtdrop_srt_kernel(tc, qT, k_words, k_scales, dm, offs, out):
                     start=True,
                     stop=True,
                 )
+        for t in range(Q_TILES):
+            for h in range(2):
+                slots = slice(h * HALF, (h + 1) * HALF)
                 nc.vector.tensor_scalar(
                     out=neg[t][:, slots],
-                    in0=bank[:, :HALF],
+                    in0=banks[t, h][:, :HALF],
                     scalar1=-1.0,
                     scalar2=neg_max[t][0][:] if h else None,
                     op0=ALU.mult,

@@ -21,6 +21,7 @@ N = 512
 HALF = N // 2
 PREFIX = T - HALF
 Q_TILES = NQ // P
+SPARE = P - 16
 
 FLOPS = 2 * NQ * N * D
 
@@ -32,9 +33,8 @@ def tile_attend_wtdrop_srt_kernel(tc, qT, k_words, k_scales, dm, offs, out):
         psum = ctx.enter_context(tc.psum_pool(name="psum", bufs=1))
 
         pool_scales = sb.tile([P, T], U8, name="pool_scales", align_bytes=64)
-        nc.scalar.dma_start(out=pool_scales[16:32, :].bitcast(I32), in_=k_scales[0].bitcast(I32))
-        for lo, hi in ((0, 16), (32, 64), (64, P)):
-            nc.vector.memset(pool_scales[lo:hi, :].bitcast(I32), 0)
+        nc.scalar.dma_start(out=pool_scales[SPARE:, :].bitcast(I32), in_=k_scales[0].bitcast(I32))
+        nc.vector.memset(pool_scales[:SPARE, :].bitcast(I32), 0)
         offsets = sb.tile([P, N // 16], U16, name="offsets")
         nc.sync.dma_start(offsets[:], offs)
         q_raw = sb.tile([P, PACK, NQ], F32, name="q_raw", tag="staged")
@@ -51,7 +51,7 @@ def tile_attend_wtdrop_srt_kernel(tc, qT, k_words, k_scales, dm, offs, out):
         nc.vector.memset(key_scales[:].bitcast(I32), 0)
         for r in range(4):
             queue = nc.scalar if r % 2 else nc.sync
-            queue.dma_start(out=key_scales[r:P:32, :].bitcast(I32), in_=spread_scales[16 + r : 32 : 4, :].bitcast(I32))
+            queue.dma_start(out=key_scales[r:P:32, :].bitcast(I32), in_=spread_scales[SPARE + r : P : 4, :].bitcast(I32))
 
         q_codes, q_scales = [], []
         for t, cast in enumerate((nc.vector.tensor_copy, nc.vector.tensor_copy)):
@@ -71,48 +71,54 @@ def tile_attend_wtdrop_srt_kernel(tc, qT, k_words, k_scales, dm, offs, out):
         nc.sync.dma_start(out=drop[:], in_=dm[0].rearrange("(t p) n -> p t n", p=P))
 
 
-        key_words = []
+        key_words = sb.tile([P, N], U32, name="key_words", align_bytes=64)
         for h, width in enumerate((PREFIX, T)):
-            kw = sb.tile([P, HALF], U32, name=f"key_words{h}", tag=f"key_words{h}", align_bytes=64)
             cols = slice(h * HALF // 16, (h + 1) * HALF // 16)
-            nc.vector.tensor_copy(kw[:], pool_words[:, :width].bitcast(U32).indirect(offsets[:, cols]))
-            key_words.append(kw)
+            nc.vector.tensor_copy(
+                key_words[:, h * HALF : (h + 1) * HALF], pool_words[:, :width].bitcast(U32).indirect(offsets[:, cols])
+            )
 
-        neg = [sb.tile([P, N], F32, name=f"neg{t}") for t in range(Q_TILES)]
-        neg_max = [[sb.tile([P, 1], F32, name=f"neg_max{t}_{h}") for h in range(2)] for t in range(Q_TILES)]
-        banks = {}
+        def scores(bank, t, slots):
+            nc.tensor.matmul_mx(
+                out=bank,
+                lhsT=q_codes[t][:].bitcast(FP8X4),
+                lhsT_scale=q_scales[t][:],
+                rhs=key_words[:, slots].bitcast(FP8X4),
+                rhs_scale=key_scales[:, slots],
+                start=True,
+                stop=True,
+            )
+
+        neg = sb.tile([P, N], F32, name="neg")
+        half_max = sb.tile([P, 1], F32, name="half_max")
+        minus_one = sb.tile([P, 1], F32, name="minus_one", tag="neg_max1")
+        nc.vector.memset(minus_one[:], -1.0)
+        neg_max = [sb.tile([P, 1], F32, name="neg_max0")]
+        halves = [psum.tile([P, HALF], F32, name=f"half{h}") for h in range(2)]
         for h in range(2):
-            slots = slice(h * HALF, (h + 1) * HALF)
-            for t in range(Q_TILES):
-                bank = psum.tile([P, N], F32, name=f"bank{t}_{h}")
-                banks[t, h] = bank
-                nc.tensor.matmul_mx(
-                    out=bank[:, :HALF],
-                    lhsT=q_codes[t][:].bitcast(FP8X4),
-                    lhsT_scale=q_scales[t][:],
-                    rhs=key_words[h][:].bitcast(FP8X4),
-                    rhs_scale=key_scales[:, slots],
-                    start=True,
-                    stop=True,
-                )
-        for t in range(Q_TILES):
-            for h in range(2):
-                slots = slice(h * HALF, (h + 1) * HALF)
-                nc.vector.tensor_scalar(
-                    out=neg[t][:, slots],
-                    in0=banks[t, h][:, :HALF],
-                    scalar1=-1.0,
-                    scalar2=neg_max[t][0][:] if h else None,
-                    op0=ALU.mult,
-                    op1=ALU.min,
-                    accum_out=neg_max[t][h][:],
-                )
+            scores(halves[h][:], 0, slice(h * HALF, (h + 1) * HALF))
+        nc.vector.tensor_reduce(half_max[:], halves[0][:], mybir.AxisListType.X, ALU.max, negate=True)
+        nc.scalar.activation(neg[:, :HALF], halves[0][:], ACT.Copy, scale=minus_one[:])
+        nc.vector.tensor_scalar(
+            out=neg[:, HALF:],
+            in0=halves[1][:],
+            scalar1=-1.0,
+            scalar2=half_max[:],
+            op0=ALU.mult,
+            op1=ALU.min,
+            accum_out=neg_max[0][:],
+        )
+        whole = psum.tile([P, N], F32, name="whole")
+        scores(whole[:], 1, slice(0, N))
+        neg_max.append(sb.tile([P, 1], F32, name="neg_max1", tag="neg_max1"))
+        nc.vector.tensor_reduce(neg_max[1][:], whole[:], mybir.AxisListType.X, ALU.max, negate=True)
 
         for t in range(Q_TILES):
             rows = slice(t * P, (t + 1) * P)
             e = sb.tile([P, N], F32, name=f"e{t}")
             row_sum = sb.tile([P, 1], F32, name=f"row_sum{t}")
-            nc.scalar.activation(e[:], neg[t][:], ACT.Exp, bias=neg_max[t][1][:], scale=-1.0, accum_out=row_sum[:])
+            source, sign = ((neg, -1.0), (whole, 1.0))[t]
+            nc.scalar.activation(e[:], source[:], ACT.Exp, bias=neg_max[t][:], scale=sign, accum_out=row_sum[:])
             inv = sb.tile([P, 1], F32, name=f"inv{t}")
             nc.vector.reciprocal(inv[:], row_sum[:])
             cuts = ((0, 192, 320, 512), (0, 128, 320, 512))[t]

@@ -95,8 +95,11 @@ def tile_attend_wtdrop_srt_kernel(tc, qT, k_words, k_scales, dm, offs, out):
         nc.vector.memset(minus_one[:], -1.0)
         neg_max = [sb.tile([P, 1], F32, name="neg_max0")]
         halves = [psum.tile([P, HALF], F32, name=f"half{h}") for h in range(2)]
+        whole = psum.tile([P, N], F32, name="whole")
         for h in range(2):
-            scores(halves[h][:], 0, slice(h * HALF, (h + 1) * HALF))
+            slots = slice(h * HALF, (h + 1) * HALF)
+            scores(halves[h][:], 0, slots)
+            scores(whole[:, slots], 1, slots)
         nc.vector.tensor_reduce(half_max[:], halves[0][:], mybir.AxisListType.X, ALU.max, negate=True)
         nc.scalar.activation(neg[:, :HALF], halves[0][:], ACT.Copy, scale=minus_one[:])
         nc.vector.tensor_scalar(
@@ -108,8 +111,6 @@ def tile_attend_wtdrop_srt_kernel(tc, qT, k_words, k_scales, dm, offs, out):
             op1=ALU.min,
             accum_out=neg_max[0][:],
         )
-        whole = psum.tile([P, N], F32, name="whole")
-        scores(whole[:], 1, slice(0, N))
         neg_max.append(sb.tile([P, 1], F32, name="neg_max1", tag="neg_max1"))
         nc.vector.tensor_reduce(neg_max[1][:], whole[:], mybir.AxisListType.X, ALU.max, negate=True)
 

@@ -32,22 +32,22 @@ def tile_attend_wtdrop_srt_kernel(tc, qT, k_words, k_scales, dm, offs, out):
         sb = ctx.enter_context(tc.tile_pool(name="sb", bufs=1))
         psum = ctx.enter_context(tc.psum_pool(name="psum", bufs=1))
 
-        pool_scales = sb.tile([P, T], U8, name="pool_scales", align_bytes=64)
+        pool_scales = sb.tile([P, T], U8, name="pool_scales", align_bytes=256)
         nc.scalar.dma_start(out=pool_scales[SPARE:, :].bitcast(I32), in_=k_scales[0].bitcast(I32))
         nc.vector.memset(pool_scales[:SPARE, :].bitcast(I32), 0)
-        offsets = sb.tile([P, N // 16], U16, name="offsets")
+        offsets = sb.tile([P, N // 16], U16, name="offsets", align_bytes=256)
         nc.sync.dma_start(offsets[:], offs)
-        q_raw = sb.tile([P, PACK, NQ], F32, name="q_raw", tag="staged")
+        q_raw = sb.tile([P, PACK, NQ], F32, name="q_raw", tag="staged", align_bytes=256)
         nc.sync.dma_start(out=q_raw[:], in_=qT[0].rearrange("(p j) w -> p j w", j=PACK))
 
-        pool_words = sb.tile([P, T], I32, name="pool_words", align_bytes=64)
+        pool_words = sb.tile([P, T], I32, name="pool_words", align_bytes=256)
         word_rows = k_words[0].rearrange("p n t -> p (n t)").bitcast(I32)
         nc.sync.dma_start(out=pool_words[:, :PREFIX], in_=word_rows[:, :PREFIX])
         nc.sync.dma_start(out=pool_words[:, PREFIX:], in_=word_rows[:, PREFIX:])
 
-        spread_scales = sb.tile([P, N], U8, name="spread_scales", align_bytes=64)
+        spread_scales = sb.tile([P, N], U8, name="spread_scales", align_bytes=256)
         nc.vector.tensor_copy(spread_scales[:], pool_scales[:].indirect(offsets[:]))
-        key_scales = sb.tile([P, N], U8, name="key_scales", align_bytes=64)
+        key_scales = sb.tile([P, N], U8, name="key_scales", align_bytes=256)
         nc.vector.memset(key_scales[:].bitcast(I32), 0)
         for r in range(4):
             queue = nc.scalar if r % 2 else nc.sync
@@ -67,7 +67,7 @@ def tile_attend_wtdrop_srt_kernel(tc, qT, k_words, k_scales, dm, offs, out):
             )
             q_codes.append(codes)
             q_scales.append(scales)
-        drop = sb.tile([P, Q_TILES, N], F32, name="drop", tag="staged")
+        drop = sb.tile([P, Q_TILES, N], F32, name="drop", tag="staged", align_bytes=256)
         nc.sync.dma_start(out=drop[:], in_=dm[0].rearrange("(t p) n -> p t n", p=P))
 
 
@@ -125,7 +125,7 @@ def tile_attend_wtdrop_srt_kernel(tc, qT, k_words, k_scales, dm, offs, out):
             cuts = ((0, 192, 320, 512), (0, 128, 320, 512))[t]
             for lo, hi in zip(cuts, cuts[1:]):
                 slots = slice(lo, hi)
-                y = sb.tile([P, hi - lo], F32, name=f"y{t}_{lo}")
+                y = sb.tile([P, hi - lo], F32, name=f"y{t}_{lo}", align_bytes=256)
                 if lo == 0:
                     kept = sb.tile([P, hi], F32, name=f"kept{t}")
                     nc.vector.tensor_tensor(kept[:], e[:, slots], drop[:, t, slots], ALU.mult)

@@ -19,7 +19,9 @@ D = 512
 NQ = 256
 N = 512
 HALF = N // 2
-PREFIX = T - HALF
+FIRST = 224
+PREFIX = T - N + FIRST
+EARLY = 192
 Q_TILES = NQ // P
 SPARE = P - 16
 
@@ -72,11 +74,9 @@ def tile_attend_wtdrop_srt_kernel(tc, qT, k_words, k_scales, dm, offs, out):
 
 
         key_words = sb.tile([P, N], U32, name="key_words", align_bytes=64)
-        for h, width in enumerate((PREFIX, T)):
-            cols = slice(h * HALF // 16, (h + 1) * HALF // 16)
-            nc.vector.tensor_copy(
-                key_words[:, h * HALF : (h + 1) * HALF], pool_words[:, :width].bitcast(U32).indirect(offsets[:, cols])
-            )
+        for lo, hi, width in ((0, FIRST, PREFIX), (FIRST, N - P, T), (N - P, N, T)):
+            window = pool_words[:, :width].bitcast(U32)
+            nc.vector.tensor_copy(key_words[:, lo:hi], window.indirect(offsets[:, lo // 16 : hi // 16]))
 
         def scores(bank, t, slots):
             nc.tensor.matmul_mx(
@@ -94,17 +94,19 @@ def tile_attend_wtdrop_srt_kernel(tc, qT, k_words, k_scales, dm, offs, out):
         minus_one = sb.tile([P, 1], F32, name="minus_one", tag="neg_max1")
         nc.vector.memset(minus_one[:], -1.0)
         neg_max = [sb.tile([P, 1], F32, name="neg_max0")]
-        halves = [psum.tile([P, HALF], F32, name=f"half{h}") for h in range(2)]
+        early = psum.tile([P, EARLY], F32, name="early")
+        late = psum.tile([P, N - EARLY], F32, name="late")
         whole = psum.tile([P, N], F32, name="whole")
-        for h in range(2):
-            slots = slice(h * HALF, (h + 1) * HALF)
-            scores(halves[h][:], 0, slots)
-            scores(whole[:, slots], 1, slots)
-        nc.vector.tensor_reduce(half_max[:], halves[0][:], mybir.AxisListType.X, ALU.max, negate=True)
-        nc.scalar.activation(neg[:, :HALF], halves[0][:], ACT.Copy, scale=minus_one[:])
+        for lo, hi in ((0, P), (P, EARLY)):
+            scores(early[:, lo:hi], 0, slice(lo, hi))
+        for lo, hi in ((EARLY, HALF), (HALF, N - P), (N - P, N)):
+            scores(late[:, lo - EARLY : hi - EARLY], 0, slice(lo, hi))
+        scores(whole[:], 1, slice(0, N))
+        nc.vector.tensor_reduce(half_max[:], early[:], mybir.AxisListType.X, ALU.max, negate=True)
+        nc.scalar.activation(neg[:, :EARLY], early[:], ACT.Copy, scale=minus_one[:])
         nc.vector.tensor_scalar(
-            out=neg[:, HALF:],
-            in0=halves[1][:],
+            out=neg[:, EARLY:],
+            in0=late[:],
             scalar1=-1.0,
             scalar2=half_max[:],
             op0=ALU.mult,

@@ -19,9 +19,9 @@ D = 512
 NQ = 256
 N = 512
 HALF = N // 2
-FIRST = 224
+FIRST = 256
 PREFIX = T - N + FIRST
-EARLY = 192
+EARLY = 256
 Q_TILES = NQ // P
 SPARE = P - 16
 
@@ -91,19 +91,24 @@ def tile_attend_wtdrop_srt_kernel(tc, qT, k_words, k_scales, dm, offs, out):
 
         neg = sb.tile([P, N], F32, name="neg")
         half_max = sb.tile([P, 1], F32, name="half_max")
-        minus_one = sb.tile([P, 1], F32, name="minus_one", tag="neg_max1")
-        nc.vector.memset(minus_one[:], -1.0)
         neg_max = [sb.tile([P, 1], F32, name="neg_max0")]
         early = psum.tile([P, EARLY], F32, name="early")
         late = psum.tile([P, N - EARLY], F32, name="late")
-        whole = psum.tile([P, N], F32, name="whole")
-        for lo, hi in ((0, P), (P, EARLY)):
-            scores(early[:, lo:hi], 0, slice(lo, hi))
-        for lo, hi in ((EARLY, HALF), (HALF, N - P), (N - P, N)):
+        early1 = psum.tile([P, P], F32, name="early1")
+        late1 = psum.tile([P, N - P], F32, name="late1")
+        neg1 = sb.tile([P, N], F32, name="neg1")
+        half_max1 = sb.tile([P, 1], F32, name="half_max1")
+        scores(early[:], 0, slice(0, EARLY))
+        scores(early1[:], 1, slice(0, P))
+        for lo, hi in ((HALF, N - P), (N - P, N)):
             scores(late[:, lo - EARLY : hi - EARLY], 0, slice(lo, hi))
-        scores(whole[:], 1, slice(0, N))
-        nc.vector.tensor_reduce(half_max[:], early[:], mybir.AxisListType.X, ALU.max, negate=True)
-        nc.scalar.activation(neg[:, :EARLY], early[:], ACT.Copy, scale=minus_one[:])
+        for lo, hi in ((P, N - P), (N - P, N)):
+            scores(late1[:, lo - P : hi - P], 1, slice(lo, hi))
+        nc.vector.tensor_scalar(
+            out=neg[:, :EARLY], in0=early[:], scalar1=-1.0, scalar2=None, op0=ALU.mult, op1=ALU.min, accum_out=half_max[:]
+        )
+        nc.vector.tensor_reduce(half_max1[:], early1[:], mybir.AxisListType.X, ALU.max, negate=True)
+        nc.scalar.activation(neg1[:, :P], early1[:], ACT.Copy, scale=-1.0)
         nc.vector.tensor_scalar(
             out=neg[:, EARLY:],
             in0=late[:],
@@ -113,14 +118,22 @@ def tile_attend_wtdrop_srt_kernel(tc, qT, k_words, k_scales, dm, offs, out):
             op1=ALU.min,
             accum_out=neg_max[0][:],
         )
-        neg_max.append(sb.tile([P, 1], F32, name="neg_max1", tag="neg_max1"))
-        nc.vector.tensor_reduce(neg_max[1][:], whole[:], mybir.AxisListType.X, ALU.max, negate=True)
+        neg_max.append(sb.tile([P, 1], F32, name="neg_max1"))
+        nc.vector.tensor_scalar(
+            out=neg1[:, P:],
+            in0=late1[:],
+            scalar1=-1.0,
+            scalar2=half_max1[:],
+            op0=ALU.mult,
+            op1=ALU.min,
+            accum_out=neg_max[1][:],
+        )
 
         for t in range(Q_TILES):
             rows = slice(t * P, (t + 1) * P)
             e = sb.tile([P, N], F32, name=f"e{t}")
             row_sum = sb.tile([P, 1], F32, name=f"row_sum{t}")
-            source, sign = ((neg, -1.0), (whole, 1.0))[t]
+            source, sign = (neg, neg1)[t], -1.0
             nc.scalar.activation(e[:], source[:], ACT.Exp, bias=neg_max[t][:], scale=sign, accum_out=row_sum[:])
             inv = sb.tile([P, 1], F32, name=f"inv{t}")
             nc.vector.reciprocal(inv[:], row_sum[:])

@@ -19,9 +19,9 @@ D = 512
 NQ = 256
 N = 512
 HALF = N // 2
-FIRST = 256
+FIRST = 224
 PREFIX = T - N + FIRST
-EARLY = 256
+EARLY = 192
 Q_TILES = NQ // P
 SPARE = P - 16
 
@@ -98,9 +98,10 @@ def tile_attend_wtdrop_srt_kernel(tc, qT, k_words, k_scales, dm, offs, out):
         late1 = psum.tile([P, N - P], F32, name="late1")
         neg1 = sb.tile([P, N], F32, name="neg1")
         half_max1 = sb.tile([P, 1], F32, name="half_max1")
-        scores(early[:], 0, slice(0, EARLY))
+        for lo, hi in ((0, P), (P, EARLY)):
+            scores(early[:, lo:hi], 0, slice(lo, hi))
         scores(early1[:], 1, slice(0, P))
-        for lo, hi in ((HALF, N - P), (N - P, N)):
+        for lo, hi in ((EARLY, HALF), (HALF, N - P), (N - P, N)):
             scores(late[:, lo - EARLY : hi - EARLY], 0, slice(lo, hi))
         for lo, hi in ((P, N - P), (N - P, N)):
             scores(late1[:, lo - P : hi - P], 1, slice(lo, hi))

from contextlib import ExitStack

import concourse.mybir as mybir

F32 = mybir.dt.float32
BF16 = mybir.dt.bfloat16
I32 = mybir.dt.int32
U32 = mybir.dt.uint32
U16 = mybir.dt.uint16
U8 = mybir.dt.uint8
FP8X4 = mybir.dt.float8_e4m3fn_x4
ALU = mybir.AluOpType
ACT = mybir.ActivationFunctionType

P = 128
PACK = 4
T = 2048
D = 512
NQ = 256
N = 512
HALF = N // 2
FIRST = 224
PREFIX = T - N + FIRST
EARLY = 192
Q_TILES = NQ // P
SPARE = P - 16

FLOPS = 2 * NQ * N * D


def tile_attend_wtdrop_srt_kernel(tc, qT, k_words, k_scales, dm, offs, out):
    nc = tc.nc
    with ExitStack() as ctx:
        sb = ctx.enter_context(tc.tile_pool(name="sb", bufs=1))
        psum = ctx.enter_context(tc.psum_pool(name="psum", bufs=1))

        pool_scales = sb.tile([P, T], U8, name="pool_scales", align_bytes=256)
        nc.scalar.dma_start(out=pool_scales[SPARE:, :].bitcast(I32), in_=k_scales[0].bitcast(I32))
        nc.vector.memset(pool_scales[:SPARE, :].bitcast(I32), 0)
        offsets = sb.tile([P, N // 16], U16, name="offsets", align_bytes=256)
        nc.sync.dma_start(offsets[:], offs)
        q_raw = sb.tile([P, PACK, NQ], F32, name="q_raw", tag="staged", align_bytes=256)
        nc.sync.dma_start(out=q_raw[:], in_=qT[0].rearrange("(p j) w -> p j w", j=PACK))

        pool_words = sb.tile([P, T], I32, name="pool_words", align_bytes=256)
        word_rows = k_words[0].rearrange("p n t -> p (n t)").bitcast(I32)
        nc.sync.dma_start(out=pool_words[:, :PREFIX], in_=word_rows[:, :PREFIX])
        nc.sync.dma_start(out=pool_words[:, PREFIX:], in_=word_rows[:, PREFIX:])

        spread_scales = sb.tile([P, N], U8, name="spread_scales", align_bytes=256)
        nc.vector.tensor_copy(spread_scales[:], pool_scales[:].indirect(offsets[:]))
        key_scales = sb.tile([P, N], U8, name="key_scales", align_bytes=256)
        nc.vector.memset(key_scales[:].bitcast(I32), 0)
        for r in range(4):
            queue = nc.scalar if r % 2 else nc.sync
            queue.dma_start(out=key_scales[r:P:32, :].bitcast(I32), in_=spread_scales[SPARE + r : P : 4, :].bitcast(I32))

        q_codes, q_scales = [], []
        for t, cast in enumerate((nc.vector.tensor_copy, nc.vector.tensor_copy)):
            q_bf = sb.tile([P, P, PACK], BF16, name=f"q_bf{t}", align_bytes=64)
            cast(
                out=q_bf[:].rearrange("p (c i) j -> p c j i", i=4),
                in_=q_raw[:, :, t * P : (t + 1) * P].rearrange("p j (c i) -> p c j i", i=4),
            )
            codes = sb.tile([P, P], U32, name=f"q_codes{t}", align_bytes=64)
            scales = sb.tile([P, P], U8, name=f"q_scales{t}", align_bytes=64)
            nc.vector.quantize_mx(
                out=codes[:].bitcast(FP8X4), scales=scales[:], in_=q_bf[:].rearrange("p w j -> p (w j)")
            )
            q_codes.append(codes)
            q_scales.append(scales)
        drop = sb.tile([P, Q_TILES, N], F32, name="drop", tag="staged", align_bytes=256)
        nc.sync.dma_start(out=drop[:], in_=dm[0].rearrange("(t p) n -> p t n", p=P))


        key_words = sb.tile([P, N], U32, name="key_words", align_bytes=64)
        for lo, hi, width in ((0, FIRST, PREFIX), (FIRST, N - P, T), (N - P, N, T)):
            window = pool_words[:, :width].bitcast(U32)
            nc.vector.tensor_copy(key_words[:, lo:hi], window.indirect(offsets[:, lo // 16 : hi // 16]))

        def scores(bank, t, slots):
            nc.tensor.matmul_mx(
                out=bank,
                lhsT=q_codes[t][:].bitcast(FP8X4),
                lhsT_scale=q_scales[t][:],
                rhs=key_words[:, slots].bitcast(FP8X4),
                rhs_scale=key_scales[:, slots],
                start=True,
                stop=True,
            )

        neg = sb.tile([P, N], F32, name="neg")
        half_max = sb.tile([P, 1], F32, name="half_max")
        neg_max = [sb.tile([P, 1], F32, name="neg_max0")]
        early = psum.tile([P, EARLY], F32, name="early")
        late = psum.tile([P, N - EARLY], F32, name="late")
        early1 = psum.tile([P, P], F32, name="early1")
        late1 = psum.tile([P, N - P], F32, name="late1")
        neg1 = sb.tile([P, N], F32, name="neg1")
        half_max1 = sb.tile([P, 1], F32, name="half_max1")
        for lo, hi in ((0, P), (P, EARLY)):
            scores(early[:, lo:hi], 0, slice(lo, hi))
        scores(early1[:], 1, slice(0, P))
        for lo, hi in ((EARLY, HALF), (HALF, N - P), (N - P, N)):
            scores(late[:, lo - EARLY : hi - EARLY], 0, slice(lo, hi))
        for lo, hi in ((P, N - P), (N - P, N)):
            scores(late1[:, lo - P : hi - P], 1, slice(lo, hi))
        nc.vector.tensor_scalar(
            out=neg[:, :EARLY], in0=early[:], scalar1=-1.0, scalar2=None, op0=ALU.mult, op1=ALU.min, accum_out=half_max[:]
        )
        nc.vector.tensor_reduce(half_max1[:], early1[:], mybir.AxisListType.X, ALU.max, negate=True)
        nc.scalar.activation(neg1[:, :P], early1[:], ACT.Copy, scale=-1.0)
        nc.vector.tensor_scalar(
            out=neg[:, EARLY:],
            in0=late[:],
            scalar1=-1.0,
            scalar2=half_max[:],
            op0=ALU.mult,
            op1=ALU.min,
            accum_out=neg_max[0][:],
        )
        neg_max.append(sb.tile([P, 1], F32, name="neg_max1"))
        nc.vector.tensor_scalar(
            out=neg1[:, P:],
            in0=late1[:],
            scalar1=-1.0,
            scalar2=half_max1[:],
            op0=ALU.mult,
            op1=ALU.min,
            accum_out=neg_max[1][:],
        )

        for t in range(Q_TILES):
            rows = slice(t * P, (t + 1) * P)
            e = sb.tile([P, N], F32, name=f"e{t}")
            row_sum = sb.tile([P, 1], F32, name=f"row_sum{t}")
            source, sign = (neg, neg1)[t], -1.0
            nc.scalar.activation(e[:], source[:], ACT.Exp, bias=neg_max[t][:], scale=sign, accum_out=row_sum[:])
            inv = sb.tile([P, 1], F32, name=f"inv{t}")
            nc.vector.reciprocal(inv[:], row_sum[:])
            cuts = ((0, 192, 320, 512), (0, 128, 320, 512))[t]
            for lo, hi in zip(cuts, cuts[1:]):
                slots = slice(lo, hi)
                y = sb.tile([P, hi - lo], F32, name=f"y{t}_{lo}", align_bytes=256)
                if lo == 0:
                    kept = sb.tile([P, hi], F32, name=f"kept{t}")
                    nc.vector.tensor_tensor(kept[:], e[:, slots], drop[:, t, slots], ALU.mult)
                    nc.scalar.activation(y[:], kept[:], ACT.Copy, scale=inv[:])
                    nc.scalar.dma_start(out=out[0, rows, slots], in_=y[:])
                else:
                    nc.vector.scalar_tensor_tensor(
                        out=y[:], in0=e[:, slots], scalar=inv[:], in1=drop[:, t, slots], op0=ALU.mult, op1=ALU.mult
                    )
                    nc.sync.dma_start(out=out[0, rows, slots], in_=y[:])
